import numpy as np
import ml_dtypes

BF16 = ml_dtypes.bfloat16


def bf(x):
    return np.asarray(x, np.float32).astype(BF16)


def f32(x):
    return np.asarray(x, np.float32)


def f64(x):
    return np.asarray(x).astype(np.float64)


def striped(idx):
    return np.tile(idx.reshape(-1, 16).T, (8, 1))


S, K, M, N, D, V = 1024, 128, 128, 256, 2, 128


def setup_inputs():
    return {"table": bf(np.random.standard_normal((K, S))), "w": bf(np.random.standard_normal((D, K, M)) / np.sqrt(D * K)), "b": f32(0.5 * np.random.standard_normal((M, 1))), "offs": striped(np.random.permutation(S)[:N])}


def reference(table, w, b, offs):
    idx = offs[:16].T.reshape(-1)
    x = f64(table)[:, idx]
    y = sum(f64(w)[t].T @ x[:, t * V : (t + 1) * V] for t in range(D))
    return np.tanh(y + f64(b))

@@ -1,0 +1,49 @@
+import concourse.mybir as mybir
+
+NODES = 1024
+FEATURES = 128
+OUTPUTS = 128
+ENDS = 2
+EDGES = 128
+LANES = 16
+
+FLOPS = 2 * ENDS * FEATURES * OUTPUTS * EDGES
+
+BF16 = mybir.dt.bfloat16
+F32 = mybir.dt.float32
+U16 = mybir.dt.uint16
+TANH = mybir.ActivationFunctionType.Tanh
+
+
+def tile_gather_matmul_kernel(tc, table, w, b, offs, out):
+    nc = tc.nc
+    offs_columns = EDGES // LANES
+
+    with (
+        tc.tile_pool(name="held", bufs=1) as held,
+        tc.psum_pool(name="psum", bufs=1) as psum,
+    ):
+        table_tile = held.tile([FEATURES, NODES], BF16)
+        offsets = held.tile([FEATURES, ENDS * offs_columns], U16)
+        weights = held.tile([FEATURES, ENDS, OUTPUTS], BF16)
+        bias = held.tile([OUTPUTS, 1], F32)
+        result = held.tile([OUTPUTS, EDGES], F32)
+        sums = psum.tile([OUTPUTS, EDGES], F32)
+
+        nc.sync.dma_start(table_tile[:], table)
+        nc.sync.dma_start(offsets[:], offs)
+        nc.scalar.dma_start(weights[:], w.rearrange("t k m -> k t m"))
+        nc.scalar.dma_start(bias[:], b)
+
+        for end in range(ENDS):
+            half = offsets[:, end * offs_columns : (end + 1) * offs_columns]
+            nc.tensor.matmul(
+                sums[:],
+                weights[:, end, :],
+                table_tile[:].indirect(half),
+                start=end == 0,
+                stop=end == ENDS - 1,
+            )
+
+        nc.scalar.activation(result[:], sums[:], TANH, bias=bias[:])
+        nc.sync.dma_start(out, result[:])

@@ -29,11 +29,16 @@ def tile_gather_matmul_kernel(tc, table, w, b, offs, out):
         bias = held.tile([OUTPUTS, 1], F32)
         result = held.tile([OUTPUTS, EDGES], F32)
         sums = psum.tile([OUTPUTS, EDGES], F32)
+        warm_in = held.tile([OUTPUTS, 1], F32)
+        warm_out = held.tile([OUTPUTS, 1], F32)
 
         nc.sync.dma_start(table_tile[:], table)
         nc.sync.dma_start(offsets[:], offs)
         nc.scalar.dma_start(weights[:], w.rearrange("t k m -> k t m"))
         nc.scalar.dma_start(bias[:], b)
+
+        nc.vector.memset(warm_in[:], 0.0)
+        nc.scalar.activation(warm_out[:], warm_in[:], TANH)
 
         for end in range(ENDS):
             half = offsets[:, end * offs_columns : (end + 1) * offs_columns]

@@ -33,9 +33,9 @@ def tile_gather_matmul_kernel(tc, table, w, b, offs, out):
         warm_out = held.tile([OUTPUTS, 1], F32)
 
         nc.sync.dma_start(table_tile[:], table)
-        nc.sync.dma_start(offsets[:], offs)
         nc.scalar.dma_start(weights[:], w.rearrange("t k m -> k t m"))
-        nc.scalar.dma_start(bias[:], b)
+        nc.sync.dma_start(offsets[:], offs)
+        nc.sync.dma_start(bias[:], b)
 
         nc.vector.memset(warm_in[:], 0.0)
         nc.scalar.activation(warm_out[:], warm_in[:], TANH)

import concourse.mybir as mybir

NODES = 1024
FEATURES = 128
OUTPUTS = 128
ENDS = 2
EDGES = 128
LANES = 16

FLOPS = 2 * ENDS * FEATURES * OUTPUTS * EDGES

BF16 = mybir.dt.bfloat16
F32 = mybir.dt.float32
U16 = mybir.dt.uint16
TANH = mybir.ActivationFunctionType.Tanh


def tile_gather_matmul_kernel(tc, table, w, b, offs, out):
    nc = tc.nc
    offs_columns = EDGES // LANES

    with (
        tc.tile_pool(name="held", bufs=1) as held,
        tc.psum_pool(name="psum", bufs=1) as psum,
    ):
        table_tile = held.tile([FEATURES, NODES], BF16)
        offsets = held.tile([FEATURES, ENDS * offs_columns], U16)
        weights = held.tile([FEATURES, ENDS, OUTPUTS], BF16)
        bias = held.tile([OUTPUTS, 1], F32)
        result = held.tile([OUTPUTS, EDGES], F32)
        sums = psum.tile([OUTPUTS, EDGES], F32)
        warm_in = held.tile([OUTPUTS, 1], F32)
        warm_out = held.tile([OUTPUTS, 1], F32)

        nc.sync.dma_start(table_tile[:], table)
        nc.scalar.dma_start(weights[:], w.rearrange("t k m -> k t m"))
        nc.sync.dma_start(offsets[:], offs)
        nc.sync.dma_start(bias[:], b)

        nc.vector.memset(warm_in[:], 0.0)
        nc.scalar.activation(warm_out[:], warm_in[:], TANH)

        for end in range(ENDS):
            half = offsets[:, end * offs_columns : (end + 1) * offs_columns]
            nc.tensor.matmul(
                sums[:],
                weights[:, end, :],
                table_tile[:].indirect(half),
                start=end == 0,
                stop=end == ENDS - 1,
            )

        nc.scalar.activation(result[:], sums[:], TANH, bias=bias[:])
        nc.sync.dma_start(out, result[:])
